import numpy as np
CORES = [0,128,256,384]
N = 4
ROUNDS = 4
def setup_inputs(rng):
    return {"x": rng.standard_normal((N, ROUNDS, 128, 128), dtype=np.float32)}
def reference(x):
    b = 128 // N
    bl = x.reshape(N, ROUNDS, 128, N, b)
    return {"y": np.ascontiguousarray(bl.transpose(3, 1, 2, 0, 4)).reshape(N, ROUNDS, 128, 128)}

@@ -1,0 +1,221 @@
+from concourse.bass import DstId, RemoteDMATransfer
+
+SPLIT = 0
+NSLOT = 3 << SPLIT
+UNITS = 2 << SPLIT
+ROWS = 512 // UNITS
+SCRATCH = {
+    "slot": ("dram", [NSLOT, 128, ROWS // 4], "float32"),
+}
+NSNT = 16
+SEMAPHORES = ["loc%d" % i for i in range(12)] + ["arr%d" % i for i in range(12)] + ["snt%d" % i for i in range(NSNT)] + ["own"]
+
+PLAN = [
+    [(0, 0, 'L', 'dL'), (0, 1, 'L', 'aR'), (0, 2, 'L', 'aL'), (1, 0, 'L', 'dR')],
+    [(0, 0, 'W', ('L', 1, 'dL')), (0, 1, 'W', ('R', 2, 'aR'))],
+    [(1, 0, 'W', ('R', 0, 'dR')), (1, 1, 'W', ('L', 1, 'rL')), (1, 2, 'S', None)],
+    [(0, 0, 'W', ('R', 1, 'rR')), (0, 2, 'W', ('L', 0, 'aL')), (0, 1, 'S', None), (1, 2, 'L', 'aL')],
+    [(1, 2, 'W', ('L', 0, 'aL')), (0, 1, 'L', 'aR'), (1, 0, 'S', None), (1, 1, 'S', None)],
+    [(0, 1, 'W', ('R', 2, 'aR')), (0, 0, 'S', None), (1, 0, 'L', 'aR'), (1, 1, 'L', 'dL')],
+    [(1, 0, 'W', ('R', 2, 'aR')), (1, 1, 'W', ('L', 1, 'dL')), (0, 0, 'L', 'dR'), (1, 2, 'S', None)],
+    [(0, 0, 'W', ('R', 1, 'dR')), (0, 1, 'W', ('L', 0, 'rL')), (0, 2, 'S', None), (1, 2, 'L', 'aR')],
+    [(1, 2, 'W', ('R', 1, 'aR')), (0, 2, 'L', 'aL'), (1, 0, 'S', None)],
+    [(0, 2, 'W', ('L', 2, 'aL')), (0, 1, 'S', None), (1, 0, 'L', 'aL')],
+    [(1, 0, 'W', ('L', 0, 'aL')), (1, 1, 'W', ('R', 2, 'rR')), (1, 2, 'S', None)],
+    [(0, 0, 'S', None), (0, 2, 'S', None)],
+]
+ORDER = ('W', 'L', 'S')
+FUSE = True
+OWN_AT = (1, 0)
+ENGINES = {1: [8], 2: [4, 4], 3: [4, 2, 2], 4: [2, 2, 2, 2]}
+
+
+def split(sched):
+    out = []
+    for acts in sched:
+        for h in (0, 1):
+            out.append([(c, 2 * i + h, op, (arg[0], 2 * arg[1] + h, arg[2]) if op == 'W' else arg) for c, i, op, arg in acts])
+    return out
+
+
+def build(sched, n, fuse=FUSE):
+    nr = 4
+    content = [[None] * n for r in range(nr)]
+    last = [[None] * n for r in range(nr)]
+    loc = [[0] * n for r in range(nr)]
+    arr = [[0] * n for r in range(nr)]
+    cnt = [dict(aR=0, aL=0, dR=0, dL=0) for r in range(nr)]
+    steps = [[] for r in range(nr)]
+    nd = sum(1 for acts in sched for a in acts if a[0] == 0 and a[2] == 'L' and a[3] == 'dR')
+    ident = 0
+    for t, acts in enumerate(sched):
+        new = []
+        for r in range(nr):
+            out = {'W': [], 'L': [], 'S': []}
+            sends = []
+            for (c, i, op, arg) in acts:
+                if c != r % 2:
+                    continue
+                if op == 'L':
+                    u = cnt[r][arg] + (nd if arg == 'dL' else 0)
+                    cnt[r][arg] += 1
+                    dest = {'aR': r + 1, 'aL': r - 1, 'dR': r + 2, 'dL': r + 2}[arg] % nr
+                    w = [] if last[r][i] is None else [last[r][i]['self']]
+                    loc[r][i] += 16
+                    sig = ('loc%d' % i, loc[r][i])
+                    out['L'].append(dict(kind='L', slot=i, dest=dest, unit=u, waits=w, sig=sig, tick=t))
+                    new.append((r, i, dict(self=sig), (r, dest, u)))
+                elif op == 'S':
+                    o, d, u = content[r][i]
+                    assert d == r
+                    loc[r][i] += 16
+                    sig = ('loc%d' % i, loc[r][i])
+                    out['S'].append(dict(kind='S', slot=i, origin=o, unit=u, waits=[last[r][i]['self']], sig=sig, tick=t))
+                    new.append((r, i, dict(self=sig), None))
+                else:
+                    sends.append((i, arg))
+            groups = [sends] if fuse else [[x] for x in sends]
+            for grp in groups:
+                if not grp:
+                    continue
+                eng = ENGINES[len(grp)]
+                ident += 1
+                trs = []
+                waits = []
+                for (i, (d, j, p)), e in zip(grp, eng):
+                    peer = (r + 1) % nr if d == 'R' else (r - 1) % nr
+                    waits.append(last[r][i]['self'])
+                    lj = last[peer][j]
+                    if lj is not None:
+                        assert lj['peer'] == r
+                        waits.append(lj['peersig'])
+                    arr[peer][j] += e
+                    sig = ('arr%d' % j, arr[peer][j])
+                    trs.append(dict(slot=i, peer=peer, pslot=j, eng=e, sig=sig, payload=content[r][i]))
+                    new.append((peer, j, dict(self=sig), content[r][i]))
+                    new.append((r, i, dict(self=('call', ident), peer=peer, peersig=sig), None))
+                out['W'].append(dict(kind='W', trs=trs, waits=waits, ident=ident, tot=sum(eng), tick=t))
+            steps[r].append(out)
+        for r, i, l, cont in new:
+            last[r][i] = l
+            content[r][i] = cont
+    return steps
+
+
+def line_up(steps, order=ORDER, own_after=OWN_AT):
+    progs = []
+    for r in range(4):
+        prog = []
+        for t, out in enumerate(steps[r]):
+            for k in order:
+                prog += out[k]
+            if t == own_after[r % 2]:
+                prog.append(dict(kind='OWN', waits=[], sig=('own', 16), tick=t))
+        progs.append(prog)
+    return progs
+
+
+def finish(prog):
+    seen = {}
+    tot = {}
+    snt = {}
+    ncall = 0
+    res = []
+    for op0 in prog:
+        op = dict(op0)
+        waits = [snt[w[1]] if w[0] == 'call' else w for w in op['waits']]
+        if op['kind'] == 'W':
+            s = 'snt%d' % (ncall % NSNT)
+            ncall += 1
+            if s in tot:
+                waits.append((s, tot[s]))
+            op['ssig'] = (s, tot.get(s, 0) + op['tot'])
+            tot[s] = op['ssig'][1]
+            snt[op['ident']] = op['ssig']
+        nw = []
+        for s, v in waits:
+            if seen.get(s, 0) < v:
+                seen[s] = v
+                nw.append((s, v))
+        op['waits'] = nw
+        if 'sig' in op:
+            tot[op['sig'][0]] = op['sig'][1]
+        res.append(op)
+    return res, seen, tot
+
+
+def programs(sched, n, order=ORDER, fuse=FUSE, own_after=OWN_AT):
+    steps = build(sched, n, fuse)
+    lined = line_up(steps, order, own_after)
+    land = [{} for r in range(4)]
+    for prog in lined:
+        for op in prog:
+            if op['kind'] == 'W':
+                for tr in op['trs']:
+                    s, v = tr['sig']
+                    land[tr['peer']][s] = max(land[tr['peer']].get(s, 0), v)
+    progs = []
+    for r in range(4):
+        res, seen, tot = finish(lined[r])
+        tot.update(land[r])
+        res.append(dict(kind='END', waits=[(s, v) for s, v in sorted(tot.items()) if seen.get(s, 0) < v], tick=999))
+        progs.append(res)
+    return progs
+
+
+def the_plan():
+    sched = PLAN
+    for k in range(SPLIT):
+        sched = split(sched)
+    own = (((OWN_AT[0] + 1) << SPLIT) - 1, ((OWN_AT[1] + 1) << SPLIT) - 1)
+    return programs(sched, NSLOT, own_after=own)
+
+
+def rank_program(g, core, T, topo):
+    rank = T.rank_of(core)
+    if rank is None:
+        return
+    sems = {"loc0": T.sem.loc0, "loc1": T.sem.loc1, "loc2": T.sem.loc2, "loc3": T.sem.loc3, "loc4": T.sem.loc4,
+            "loc5": T.sem.loc5, "loc6": T.sem.loc6, "loc7": T.sem.loc7, "loc8": T.sem.loc8, "loc9": T.sem.loc9,
+            "loc10": T.sem.loc10, "loc11": T.sem.loc11, "arr0": T.sem.arr0, "arr1": T.sem.arr1, "arr2": T.sem.arr2,
+            "arr3": T.sem.arr3, "arr4": T.sem.arr4, "arr5": T.sem.arr5, "arr6": T.sem.arr6, "arr7": T.sem.arr7,
+            "arr8": T.sem.arr8, "arr9": T.sem.arr9, "arr10": T.sem.arr10, "arr11": T.sem.arr11, "snt0": T.sem.snt0,
+            "snt1": T.sem.snt1, "snt2": T.sem.snt2, "snt3": T.sem.snt3, "snt4": T.sem.snt4, "snt5": T.sem.snt5,
+            "snt6": T.sem.snt6, "snt7": T.sem.snt7, "snt8": T.sem.snt8, "snt9": T.sem.snt9, "snt10": T.sem.snt10,
+            "snt11": T.sem.snt11, "snt12": T.sem.snt12, "snt13": T.sem.snt13, "snt14": T.sem.snt14, "snt15": T.sem.snt15,
+            "own": T.sem.own}
+
+    def piece(t, blk, unit):
+        c0, c1 = blk * 32, (blk + 1) * 32
+        r0 = unit * ROWS
+        if ROWS > 128:
+            return t[r0 // 128:(r0 + ROWS) // 128, :, c0:c1]
+        return t[r0 // 128, r0 % 128:r0 % 128 + ROWS, c0:c1]
+
+    for op in the_plan()[rank]:
+        for s, v in op['waits']:
+            g.wait_ge(sems[s], v)
+        kind = op['kind']
+        if kind == 'L':
+            g.dma_start(T.slot[op['slot']], piece(T.x, op['dest'], op['unit'])).then_inc(sems[op['sig'][0]], 16)
+        elif kind == 'S':
+            g.dma_start(piece(T.y, op['origin'], op['unit']), T.slot[op['slot']]).then_inc(sems[op['sig'][0]], 16)
+        elif kind == 'OWN':
+            c0, c1 = rank * 32, (rank + 1) * 32
+            g.dma_start(T.y[:, :, c0:c1], T.x[:, :, c0:c1]).then_inc(sems['own'], 16)
+        elif kind == 'W':
+            snt = sems[op['ssig'][0]]
+            trs = []
+            bit = 0
+            for tr in op['trs']:
+                rid, pid = topo.addr(T.cores[tr['peer']], core)
+                trs.append((rid, pid, ((1 << tr['eng']) - 1) << bit, tr))
+                bit += tr['eng']
+            if len(trs) == 1:
+                rid, pid, mask, tr = trs[0]
+                g.remote_dma(T.slot[tr['pslot']], T.slot[tr['slot']], sems[tr['sig'][0]], snt, pid, rid, mask)
+            else:
+                g.remote_dma_fused(
+                    [RemoteDMATransfer(dst_ids=[DstId(rid=rid, pnc=pid)], dma_engine_mask=mask, remote_sem=sems[tr['sig'][0]],
+                                       src=T.slot[tr['slot']], dst=T.slot[tr['pslot']]) for rid, pid, mask, tr in trs],
+                    local_sem=snt)

@@ -1,6 +1,6 @@
 from concourse.bass import DstId, RemoteDMATransfer
 
-SPLIT = 0
+SPLIT = 1
 NSLOT = 3 << SPLIT
 UNITS = 2 << SPLIT
 ROWS = 512 // UNITS
@@ -217,5 +217,6 @@ def rank_program(g, core, T, topo):
             else:
                 g.remote_dma_fused(
                     [RemoteDMATransfer(dst_ids=[DstId(rid=rid, pnc=pid)], dma_engine_mask=mask, remote_sem=sems[tr['sig'][0]],
-                                       src=T.slot[tr['slot']], dst=T.slot[tr['pslot']]) for rid, pid, mask, tr in trs],
+                                       src=T.slot[tr['slot']], dst=T.slot[tr['slot']] if False else T.slot[tr['pslot']])
+                     for rid, pid, mask, tr in trs],
                     local_sem=snt)

@@ -7,8 +7,8 @@ ROWS = 512 // UNITS
 SCRATCH = {
     "slot": ("dram", [NSLOT, 128, ROWS // 4], "float32"),
 }
-NSNT = 16
-SEMAPHORES = ["loc%d" % i for i in range(12)] + ["arr%d" % i for i in range(12)] + ["snt%d" % i for i in range(NSNT)] + ["own"]
+NSNT = 10
+SEMAPHORES = ["loc%d" % i for i in range(6)] + ["arr%d" % i for i in range(6)] + ["snt%d" % i for i in range(NSNT)] + ["own"]
 
 PLAN = [
     [(0, 0, 'L', 'dL'), (0, 1, 'L', 'aR'), (0, 2, 'L', 'aL'), (1, 0, 'L', 'dR')],
@@ -25,9 +25,8 @@ PLAN = [
     [(0, 0, 'S', None), (0, 2, 'S', None)],
 ]
 ORDER = ('W', 'L', 'S')
-FUSE = True
 OWN_AT = (1, 0)
-ENGINES = {1: [8], 2: [4, 4], 3: [4, 2, 2], 4: [2, 2, 2, 2]}
+ENGINES = {1: [8], 2: [4, 4]}
 
 
 def split(sched):
@@ -38,7 +37,7 @@ def split(sched):
     return out
 
 
-def build(sched, n, fuse=FUSE):
+def build(sched, n):
     nr = 4
     content = [[None] * n for r in range(nr)]
     last = [[None] * n for r in range(nr)]
@@ -74,15 +73,12 @@ def build(sched, n, fuse=FUSE):
                     new.append((r, i, dict(self=sig), None))
                 else:
                     sends.append((i, arg))
-            groups = [sends] if fuse else [[x] for x in sends]
-            for grp in groups:
-                if not grp:
-                    continue
-                eng = ENGINES[len(grp)]
+            if sends:
+                eng = ENGINES[len(sends)]
                 ident += 1
                 trs = []
                 waits = []
-                for (i, (d, j, p)), e in zip(grp, eng):
+                for (i, (d, j, p)), e in zip(sends, eng):
                     peer = (r + 1) % nr if d == 'R' else (r - 1) % nr
                     waits.append(last[r][i]['self'])
                     lj = last[peer][j]
@@ -102,7 +98,7 @@ def build(sched, n, fuse=FUSE):
     return steps
 
 
-def line_up(steps, order=ORDER, own_after=OWN_AT):
+def line_up(steps, order, own_after):
     progs = []
     for r in range(4):
         prog = []
@@ -144,9 +140,8 @@ def finish(prog):
     return res, seen, tot
 
 
-def programs(sched, n, order=ORDER, fuse=FUSE, own_after=OWN_AT):
-    steps = build(sched, n, fuse)
-    lined = line_up(steps, order, own_after)
+def programs(sched, n, order=ORDER, own_after=OWN_AT):
+    lined = line_up(build(sched, n), order, own_after)
     land = [{} for r in range(4)]
     for prog in lined:
         for op in prog:
@@ -176,14 +171,10 @@ def rank_program(g, core, T, topo):
     if rank is None:
         return
     sems = {"loc0": T.sem.loc0, "loc1": T.sem.loc1, "loc2": T.sem.loc2, "loc3": T.sem.loc3, "loc4": T.sem.loc4,
-            "loc5": T.sem.loc5, "loc6": T.sem.loc6, "loc7": T.sem.loc7, "loc8": T.sem.loc8, "loc9": T.sem.loc9,
-            "loc10": T.sem.loc10, "loc11": T.sem.loc11, "arr0": T.sem.arr0, "arr1": T.sem.arr1, "arr2": T.sem.arr2,
-            "arr3": T.sem.arr3, "arr4": T.sem.arr4, "arr5": T.sem.arr5, "arr6": T.sem.arr6, "arr7": T.sem.arr7,
-            "arr8": T.sem.arr8, "arr9": T.sem.arr9, "arr10": T.sem.arr10, "arr11": T.sem.arr11, "snt0": T.sem.snt0,
-            "snt1": T.sem.snt1, "snt2": T.sem.snt2, "snt3": T.sem.snt3, "snt4": T.sem.snt4, "snt5": T.sem.snt5,
-            "snt6": T.sem.snt6, "snt7": T.sem.snt7, "snt8": T.sem.snt8, "snt9": T.sem.snt9, "snt10": T.sem.snt10,
-            "snt11": T.sem.snt11, "snt12": T.sem.snt12, "snt13": T.sem.snt13, "snt14": T.sem.snt14, "snt15": T.sem.snt15,
-            "own": T.sem.own}
+            "loc5": T.sem.loc5, "arr0": T.sem.arr0, "arr1": T.sem.arr1, "arr2": T.sem.arr2, "arr3": T.sem.arr3,
+            "arr4": T.sem.arr4, "arr5": T.sem.arr5, "snt0": T.sem.snt0, "snt1": T.sem.snt1, "snt2": T.sem.snt2,
+            "snt3": T.sem.snt3, "snt4": T.sem.snt4, "snt5": T.sem.snt5, "snt6": T.sem.snt6, "snt7": T.sem.snt7,
+            "snt8": T.sem.snt8, "snt9": T.sem.snt9, "own": T.sem.own}
 
     def piece(t, blk, unit):
         c0, c1 = blk * 32, (blk + 1) * 32
@@ -217,6 +208,5 @@ def rank_program(g, core, T, topo):
             else:
                 g.remote_dma_fused(
                     [RemoteDMATransfer(dst_ids=[DstId(rid=rid, pnc=pid)], dma_engine_mask=mask, remote_sem=sems[tr['sig'][0]],
-                                       src=T.slot[tr['slot']], dst=T.slot[tr['slot']] if False else T.slot[tr['pslot']])
-                     for rid, pid, mask, tr in trs],
+                                       src=T.slot[tr['slot']], dst=T.slot[tr['pslot']]) for rid, pid, mask, tr in trs],
                     local_sem=snt)

from concourse.bass import DstId, RemoteDMATransfer

SPLIT = 1
NSLOT = 3 << SPLIT
UNITS = 2 << SPLIT
ROWS = 512 // UNITS
SCRATCH = {
    "slot": ("dram", [NSLOT, 128, ROWS // 4], "float32"),
}
NSNT = 10
SEMAPHORES = ["loc%d" % i for i in range(6)] + ["arr%d" % i for i in range(6)] + ["snt%d" % i for i in range(NSNT)] + ["own"]

PLAN = [
    [(0, 0, 'L', 'dL'), (0, 1, 'L', 'aR'), (0, 2, 'L', 'aL'), (1, 0, 'L', 'dR')],
    [(0, 0, 'W', ('L', 1, 'dL')), (0, 1, 'W', ('R', 2, 'aR'))],
    [(1, 0, 'W', ('R', 0, 'dR')), (1, 1, 'W', ('L', 1, 'rL')), (1, 2, 'S', None)],
    [(0, 0, 'W', ('R', 1, 'rR')), (0, 2, 'W', ('L', 0, 'aL')), (0, 1, 'S', None), (1, 2, 'L', 'aL')],
    [(1, 2, 'W', ('L', 0, 'aL')), (0, 1, 'L', 'aR'), (1, 0, 'S', None), (1, 1, 'S', None)],
    [(0, 1, 'W', ('R', 2, 'aR')), (0, 0, 'S', None), (1, 0, 'L', 'aR'), (1, 1, 'L', 'dL')],
    [(1, 0, 'W', ('R', 2, 'aR')), (1, 1, 'W', ('L', 1, 'dL')), (0, 0, 'L', 'dR'), (1, 2, 'S', None)],
    [(0, 0, 'W', ('R', 1, 'dR')), (0, 1, 'W', ('L', 0, 'rL')), (0, 2, 'S', None), (1, 2, 'L', 'aR')],
    [(1, 2, 'W', ('R', 1, 'aR')), (0, 2, 'L', 'aL'), (1, 0, 'S', None)],
    [(0, 2, 'W', ('L', 2, 'aL')), (0, 1, 'S', None), (1, 0, 'L', 'aL')],
    [(1, 0, 'W', ('L', 0, 'aL')), (1, 1, 'W', ('R', 2, 'rR')), (1, 2, 'S', None)],
    [(0, 0, 'S', None), (0, 2, 'S', None)],
]
ORDER = ('W', 'L', 'S')
OWN_AT = (1, 0)
ENGINES = {1: [8], 2: [4, 4]}


def split(sched):
    out = []
    for acts in sched:
        for h in (0, 1):
            out.append([(c, 2 * i + h, op, (arg[0], 2 * arg[1] + h, arg[2]) if op == 'W' else arg) for c, i, op, arg in acts])
    return out


def build(sched, n):
    nr = 4
    content = [[None] * n for r in range(nr)]
    last = [[None] * n for r in range(nr)]
    loc = [[0] * n for r in range(nr)]
    arr = [[0] * n for r in range(nr)]
    cnt = [dict(aR=0, aL=0, dR=0, dL=0) for r in range(nr)]
    steps = [[] for r in range(nr)]
    nd = sum(1 for acts in sched for a in acts if a[0] == 0 and a[2] == 'L' and a[3] == 'dR')
    ident = 0
    for t, acts in enumerate(sched):
        new = []
        for r in range(nr):
            out = {'W': [], 'L': [], 'S': []}
            sends = []
            for (c, i, op, arg) in acts:
                if c != r % 2:
                    continue
                if op == 'L':
                    u = cnt[r][arg] + (nd if arg == 'dL' else 0)
                    cnt[r][arg] += 1
                    dest = {'aR': r + 1, 'aL': r - 1, 'dR': r + 2, 'dL': r + 2}[arg] % nr
                    w = [] if last[r][i] is None else [last[r][i]['self']]
                    loc[r][i] += 16
                    sig = ('loc%d' % i, loc[r][i])
                    out['L'].append(dict(kind='L', slot=i, dest=dest, unit=u, waits=w, sig=sig, tick=t))
                    new.append((r, i, dict(self=sig), (r, dest, u)))
                elif op == 'S':
                    o, d, u = content[r][i]
                    assert d == r
                    loc[r][i] += 16
                    sig = ('loc%d' % i, loc[r][i])
                    out['S'].append(dict(kind='S', slot=i, origin=o, unit=u, waits=[last[r][i]['self']], sig=sig, tick=t))
                    new.append((r, i, dict(self=sig), None))
                else:
                    sends.append((i, arg))
            if sends:
                eng = ENGINES[len(sends)]
                ident += 1
                trs = []
                waits = []
                for (i, (d, j, p)), e in zip(sends, eng):
                    peer = (r + 1) % nr if d == 'R' else (r - 1) % nr
                    waits.append(last[r][i]['self'])
                    lj = last[peer][j]
                    if lj is not None:
                        assert lj['peer'] == r
                        waits.append(lj['peersig'])
                    arr[peer][j] += e
                    sig = ('arr%d' % j, arr[peer][j])
                    trs.append(dict(slot=i, peer=peer, pslot=j, eng=e, sig=sig, payload=content[r][i]))
                    new.append((peer, j, dict(self=sig), content[r][i]))
                    new.append((r, i, dict(self=('call', ident), peer=peer, peersig=sig), None))
                out['W'].append(dict(kind='W', trs=trs, waits=waits, ident=ident, tot=sum(eng), tick=t))
            steps[r].append(out)
        for r, i, l, cont in new:
            last[r][i] = l
            content[r][i] = cont
    return steps


def line_up(steps, order, own_after):
    progs = []
    for r in range(4):
        prog = []
        for t, out in enumerate(steps[r]):
            for k in order:
                prog += out[k]
            if t == own_after[r % 2]:
                prog.append(dict(kind='OWN', waits=[], sig=('own', 16), tick=t))
        progs.append(prog)
    return progs


def finish(prog):
    seen = {}
    tot = {}
    snt = {}
    ncall = 0
    res = []
    for op0 in prog:
        op = dict(op0)
        waits = [snt[w[1]] if w[0] == 'call' else w for w in op['waits']]
        if op['kind'] == 'W':
            s = 'snt%d' % (ncall % NSNT)
            ncall += 1
            if s in tot:
                waits.append((s, tot[s]))
            op['ssig'] = (s, tot.get(s, 0) + op['tot'])
            tot[s] = op['ssig'][1]
            snt[op['ident']] = op['ssig']
        nw = []
        for s, v in waits:
            if seen.get(s, 0) < v:
                seen[s] = v
                nw.append((s, v))
        op['waits'] = nw
        if 'sig' in op:
            tot[op['sig'][0]] = op['sig'][1]
        res.append(op)
    return res, seen, tot


def programs(sched, n, order=ORDER, own_after=OWN_AT):
    lined = line_up(build(sched, n), order, own_after)
    land = [{} for r in range(4)]
    for prog in lined:
        for op in prog:
            if op['kind'] == 'W':
                for tr in op['trs']:
                    s, v = tr['sig']
                    land[tr['peer']][s] = max(land[tr['peer']].get(s, 0), v)
    progs = []
    for r in range(4):
        res, seen, tot = finish(lined[r])
        tot.update(land[r])
        res.append(dict(kind='END', waits=[(s, v) for s, v in sorted(tot.items()) if seen.get(s, 0) < v], tick=999))
        progs.append(res)
    return progs


def the_plan():
    sched = PLAN
    for k in range(SPLIT):
        sched = split(sched)
    own = (((OWN_AT[0] + 1) << SPLIT) - 1, ((OWN_AT[1] + 1) << SPLIT) - 1)
    return programs(sched, NSLOT, own_after=own)


def rank_program(g, core, T, topo):
    rank = T.rank_of(core)
    if rank is None:
        return
    sems = {"loc0": T.sem.loc0, "loc1": T.sem.loc1, "loc2": T.sem.loc2, "loc3": T.sem.loc3, "loc4": T.sem.loc4,
            "loc5": T.sem.loc5, "arr0": T.sem.arr0, "arr1": T.sem.arr1, "arr2": T.sem.arr2, "arr3": T.sem.arr3,
            "arr4": T.sem.arr4, "arr5": T.sem.arr5, "snt0": T.sem.snt0, "snt1": T.sem.snt1, "snt2": T.sem.snt2,
            "snt3": T.sem.snt3, "snt4": T.sem.snt4, "snt5": T.sem.snt5, "snt6": T.sem.snt6, "snt7": T.sem.snt7,
            "snt8": T.sem.snt8, "snt9": T.sem.snt9, "own": T.sem.own}

    def piece(t, blk, unit):
        c0, c1 = blk * 32, (blk + 1) * 32
        r0 = unit * ROWS
        if ROWS > 128:
            return t[r0 // 128:(r0 + ROWS) // 128, :, c0:c1]
        return t[r0 // 128, r0 % 128:r0 % 128 + ROWS, c0:c1]

    for op in the_plan()[rank]:
        for s, v in op['waits']:
            g.wait_ge(sems[s], v)
        kind = op['kind']
        if kind == 'L':
            g.dma_start(T.slot[op['slot']], piece(T.x, op['dest'], op['unit'])).then_inc(sems[op['sig'][0]], 16)
        elif kind == 'S':
            g.dma_start(piece(T.y, op['origin'], op['unit']), T.slot[op['slot']]).then_inc(sems[op['sig'][0]], 16)
        elif kind == 'OWN':
            c0, c1 = rank * 32, (rank + 1) * 32
            g.dma_start(T.y[:, :, c0:c1], T.x[:, :, c0:c1]).then_inc(sems['own'], 16)
        elif kind == 'W':
            snt = sems[op['ssig'][0]]
            trs = []
            bit = 0
            for tr in op['trs']:
                rid, pid = topo.addr(T.cores[tr['peer']], core)
                trs.append((rid, pid, ((1 << tr['eng']) - 1) << bit, tr))
                bit += tr['eng']
            if len(trs) == 1:
                rid, pid, mask, tr = trs[0]
                g.remote_dma(T.slot[tr['pslot']], T.slot[tr['slot']], sems[tr['sig'][0]], snt, pid, rid, mask)
            else:
                g.remote_dma_fused(
                    [RemoteDMATransfer(dst_ids=[DstId(rid=rid, pnc=pid)], dma_engine_mask=mask, remote_sem=sems[tr['sig'][0]],
                                       src=T.slot[tr['slot']], dst=T.slot[tr['pslot']]) for rid, pid, mask, tr in trs],
                    local_sem=snt)
